import numpy as np, ml_dtypes
CORES = [1,17,65,89,97,113]
N = 6
import mx_ref
NC, KT, G, WT = 128, 1, 4, 2
C = np.float32(0.037)
BF = ml_dtypes.bfloat16
def cut(t, i, w=512):
    return t[:, w * i:w * i + w]
def tile(rs):
    return np.stack(rs, axis=2).reshape(128, -1).astype(BF)
def layer(w, X):
    out = []
    for i in range(G):
        for t in range(len(X)):
            p = mx_ref.matmul(mx_ref.quantize(cut(w, len(X) * i + t)), X[t])
            z = p if t == 0 else z + p
        out.append(z)
    return out
def act(Z):
    return [np.maximum(z, 0) * C for z in Z]
def setup_inputs(rng):
    def f(*shape):
        return mx_ref.flush((rng.standard_normal(shape, dtype=np.float32) * np.exp2(rng.integers(-2, 3, shape[:-1] + (1,)))).astype(BF))
    return {"x": f(N, 128, KT * 4 * NC), "w1": f(N, 128, G * KT * 512), "w2": f(N, 128, WT * 512)}
def setup_inputs_blocks(rng):
    d = setup_inputs(rng)
    for k in ("x", "w1", "w2"): d[k] = mx_ref.spread(d[k], rng, 4)
    return d
def setup_inputs_wide(rng):
    d = setup_inputs(rng)
    for k in ("x", "w1", "w2"): d[k] = mx_ref.flush((d[k].astype(np.float32) * np.exp2(rng.integers(-8, 9, (N, 1, 1))).astype(np.float32)).astype(BF))
    return d
def setup_inputs_zeros(rng):
    d = setup_inputs(rng); v = d["x"].reshape(N, 128, -1, 4).copy()
    v[np.broadcast_to((rng.random((N, 1, v.shape[2], 1)) < 0.33), v.shape)] = 0
    d["x"] = v.reshape(d["x"].shape)
    return d
def reference(x, w1, w2):
    H = [mx_ref.quantize(tile(act(layer(w1[j], [mx_ref.quantize(cut(x[j], t, 4 * NC)) for t in range(KT)])))) for j in range(N)]
    y = np.zeros((N, 128, N * WT * NC), np.float32)
    for r in range(N):
        for i in range(WT):
            qw = mx_ref.quantize(cut(w2[r], i))
            for j in range(N):
                y[r][:, NC * (WT * j + i):NC * (WT * j + i) + NC] = mx_ref.matmul(qw, H[j])
    return {"y": y}

@@ -1,0 +1,228 @@
+from concourse.bass import DstId, RemoteDMATransfer
+from concourse.mybir import dt, AluOpType, ActivationFunctionType
+
+N = 6
+NC = 128
+TW = 4 * NC
+G = 4
+WT = 2
+C = 0.037
+BANK = 512
+NBANK = 8
+
+SCRATCH = {
+    "xb": ("sbuf", [128, TW], "bfloat16"),
+    "w1b": ("sbuf", [128, G * TW], "bfloat16"),
+    "w2b": ("sbuf", [128, WT * TW], "bfloat16"),
+    "hb": ("sbuf", [128, TW], "bfloat16"),
+    "xq": ("sbuf", [128, NC], "float8_e4m3fn_x4"),
+    "xs": ("sbuf", [128, NC], "uint8"),
+    "w1q": ("sbuf", [128, G * NC], "float8_e4m3fn_x4"),
+    "w1s": ("sbuf", [128, G * NC], "uint8"),
+    "w2q": ("sbuf", [128, WT * NC], "float8_e4m3fn_x4"),
+    "w2s": ("sbuf", [128, WT * NC], "uint8"),
+    "hq": ("sbuf", [128, N * NC], "float8_e4m3fn_x4"),
+    "hs": ("sbuf", [128, N * NC], "uint8"),
+    "ps": ("psum", [128, NBANK * BANK], "float32"),
+    "yb": ("sbuf", [128, N * WT * NC], "float32"),
+}
+SEMAPHORES = (
+    ["lx", "lw1a", "lw1b", "lw2", "qx", "qh", "qv", "rc", "rs", "ls", "sta", "stb"]
+    + ["qw%d" % i for i in range(G)] + ["m%d" % i for i in range(G)] + ["a%d" % i for i in range(G)]
+    + ["arr%d" % j for j in range(N)]
+    + ["n%d_%d" % (k, i) for k in range(N) for i in range(WT)]
+    + ["c%d_%d" % (k, i) for k in range(N) for i in range(WT)]
+)
+
+PARTS = ("c", "s")
+WEIGHT = {"c": 3, "s": 2}
+
+
+def _count(mask):
+    return bin(mask).count("1")
+
+
+def _plan(cores, topo):
+    n = len(cores)
+    every = range(topo.CHIPS * topo.CORES_PER_CHIP)
+    plan = []
+    for j, s in enumerate(cores):
+        others = sorted((d for d in range(n) if d != j), key=lambda d: (d - j) % n)
+        direct = [d for d in others if topo.may_write(s, cores[d])]
+        far = [d for d in others if not topo.may_write(s, cores[d])]
+        jobs = {}
+        if far:
+            cand = [c for c in every if topo.chip(c) == topo.chip(s) and c not in cores
+                    and all(topo.may_write(c, cores[d]) for d in far)]
+            near = [c for c in cand if topo.die(c) == topo.die(s)]
+            away = [c for c in cand if topo.die(c) != topo.die(s)]
+            units = [(p, d) for p in PARTS for d in far]
+            if len(units) <= len(near):
+                use = near
+                if len(units) <= len(away) and _late(cores, topo, j, far[0]):
+                    use = away
+                helpers = use[:len(units)]
+            else:
+                helpers = []
+                for k in range(max(len(near), len(away))):
+                    helpers += near[k:k + 1] + away[k:k + 1]
+            target = sum(WEIGHT[p] for p, d in units) / len(helpers)
+            k, load = 0, 0
+            for p, d in units:
+                if k < len(helpers) - 1 and load > 0 and load + WEIGHT[p] / 2 > target:
+                    k, load = k + 1, 0
+                jobs.setdefault(helpers[k], {q: [] for q in PARTS})[p].append(d)
+                load += WEIGHT[p]
+        plan.append({"direct": direct, "far": far, "jobs": jobs})
+    return plan
+
+
+def _peers(cores, topo, d):
+    n = len(cores)
+    return sorted((t for t in range(n) if t != d and not topo.may_write(cores[t], cores[d])), key=lambda t: (d - t) % n)
+
+
+def _late(cores, topo, j, d):
+    peers = _peers(cores, topo, d)
+    return peers.index(j) >= (len(peers) + 1) // 2
+
+
+def _order(cores, topo, plan, r):
+    direct = sorted((t for t in range(len(cores)) if r in plan[t]["direct"]), key=lambda t: plan[t]["direct"].index(r))
+    return [r] + direct + _peers(cores, topo, r)
+
+
+def rank_program(g, core, T, topo):
+    cores = [int(c) for c in T.cores]
+    plan = _plan(cores, topo)
+    S = T.sem
+
+    def view(part, j):
+        if part == "c":
+            return T.hq[:, NC * j:NC * (j + 1)].bitcast(dt.uint8)
+        return T.hs[:, NC * j:NC * (j + 1)]
+
+    def common_mask(src, dst):
+        m = None
+        for d in dst:
+            m = topo.mask(src, d) if m is None else m & topo.mask(src, d)
+        return m
+
+    def send(part, j, dst, mask, sem):
+        ids = []
+        for d in dst:
+            a = topo.addr(d)
+            ids.append(DstId(rid=a[0], pnc=a[1]))
+        g.remote_dma_fused([RemoteDMATransfer(dst_ids=ids, dma_engine_mask=mask, remote_sem=sem,
+                                              srcs=[view(part, j)], dsts=[view(part, j) for d in dst])],
+                           local_sem=S.ls)
+        return _count(mask)
+
+    def hop1_mask(j):
+        busy = 0
+        for d in plan[j]["direct"]:
+            busy |= topo.mask(cores[j], cores[d])
+        return common_mask(cores[j], list(plan[j]["jobs"])) & ~busy
+
+    for j in range(N):
+        if core in plan[j]["jobs"]:
+            job = plan[j]["jobs"][core]
+            left = 0
+            for p in PARTS:
+                if job[p]:
+                    dst = [cores[d] for d in job[p]]
+                    g.wait_ge(S.rc if p == "c" else S.rs, _count(hop1_mask(j)))
+                    left += send(p, j, dst, common_mask(core, dst), S["arr%d" % j])
+            g.wait_ge(S.ls, left)
+            return
+
+    r = T.rank_of(core)
+    if r is None:
+        return
+    v, t, a, q = g.vector, g.tensor, g.scalar, g.sync
+
+    def bank(b):
+        return T.ps[:, BANK * b:BANK * b + NC]
+
+    head = (G - 1) * TW
+    q.dma_start(T.xb[:], T.x[:]).then_inc(S.lx, 16)
+    a.dma_start(T.w1b[:, 0:head], T.w1[:, 0:head]).then_inc(S.lw1a, 16)
+    q.dma_start(T.w1b[:, head:G * TW], T.w1[:, head:G * TW]).then_inc(S.lw1b, 16)
+    q.dma_start(T.w2b[:], T.w2[:]).then_inc(S.lw2, 16)
+
+    v.wait_ge(S.lx, 16)
+    v.quantize_mx(T.xq[:], T.xs[:], T.xb[:]).then_inc(S.qx, 1)
+    t.wait_ge(S.qx, 1)
+    for i in range(G):
+        if i == 0:
+            v.wait_ge(S.lw1a, 16)
+        if i == G - 1:
+            v.wait_ge(S.lw1b, 16)
+        cols = slice(NC * i, NC * (i + 1))
+        v.quantize_mx(T.w1q[:, cols], T.w1s[:, cols], T.w1b[:, TW * i:TW * (i + 1)]).then_inc(S["qw%d" % i], 1)
+        t.wait_ge(S["qw%d" % i], 1)
+        t.matmul_mx(bank(i), T.w1q[:, cols], T.w1s[:, cols], T.xq[:], T.xs[:], True, True).then_inc(S["m%d" % i], 1)
+        if i < G - 1:
+            a.wait_ge(S["m%d" % i], 1)
+            a.activation(T.hb[:, i:TW:4], bank(i), ActivationFunctionType.Relu, scale=C).then_inc(S["a%d" % i], 1)
+        else:
+            v.wait_ge(S["m%d" % i], 1)
+            v.tensor_scalar(T.hb[:, i:TW:4], bank(i), 0.0, C, AluOpType.max, AluOpType.mult).then_inc(S["a%d" % i], 1)
+    for i in range(G):
+        v.wait_ge(S["a%d" % i], 1)
+    own = slice(NC * r, NC * (r + 1))
+    v.quantize_mx(T.hq[:, own], T.hs[:, own], T.hb[:]).then_inc(S.qh, 1)
+    v.wait_ge(S.lw2, 16)
+    v.quantize_mx(T.w2q[:], T.w2s[:], T.w2b[:]).then_inc(S.qv, 1)
+
+    g.wait_ge(S.qh, 1)
+    left = 0
+    jobs = plan[r]["jobs"]
+    for p in PARTS:
+        to = [h for h in jobs if jobs[h][p]]
+        if to:
+            left += send(p, r, to, hop1_mask(r), S.rc if p == "c" else S.rs)
+    direct = [cores[d] for d in plan[r]["direct"]]
+    if direct:
+        for p in reversed(PARTS):
+            left += send(p, r, direct, common_mask(core, direct), S["arr%d" % r])
+    g.wait_ge(S.ls, left)
+
+    stores = {"sta": 0, "stb": 0}
+    t.wait_ge(S.qv, 1)
+    for k, j in enumerate(_order(cores, topo, plan, r)):
+        if j == r:
+            t.wait_ge(S.qh, 1)
+        else:
+            if r in plan[j]["direct"]:
+                n_in = len(PARTS) * _count(common_mask(cores[j], [cores[d] for d in plan[j]["direct"]]))
+            else:
+                n_in = sum(_count(common_mask(h, [cores[d] for d in plan[j]["jobs"][h][p]]))
+                           for h in plan[j]["jobs"] for p in PARTS if r in plan[j]["jobs"][h][p])
+            t.wait_ge(S["arr%d" % j], n_in)
+        slot = slice(NC * j, NC * (j + 1))
+        for i in range(WT):
+            b = (G + WT * k + i) % NBANK
+            if G + WT * k + i >= NBANK:
+                if WT * k + i < NBANK:
+                    t.wait_ge(S["a%d" % b], 1)
+                else:
+                    t.wait_ge(S["c%d_%d" % ((WT * k + i - NBANK) // WT, i)], 1)
+            w = slice(NC * i, NC * (i + 1))
+            t.matmul_mx(bank(b), T.w2q[:, w], T.w2s[:, w], T.hq[:, slot], T.hs[:, slot], True, True
+                        ).then_inc(S["n%d_%d" % (k, i)], 1)
+            out = T.yb[:, NC * (WT * j + i):NC * (WT * j + i + 1)]
+            if i == 0:
+                v.wait_ge(S["n%d_%d" % (k, i)], 1)
+                v.tensor_copy(out, bank(b)).then_inc(S["c%d_%d" % (k, i)], 1)
+            else:
+                a.wait_ge(S["n%d_%d" % (k, i)], 1)
+                a.activation(out, bank(b), ActivationFunctionType.Copy).then_inc(S["c%d_%d" % (k, i)], 1)
+        e, name = (q, "sta") if k % 2 == 0 else (a, "stb")
+        for i in range(WT):
+            e.wait_ge(S["c%d_%d" % (k, i)], 1)
+        blk = slice(NC * WT * j, NC * WT * (j + 1))
+        e.dma_start(T.y[:, blk], T.yb[:, blk]).then_inc(S[name], 16)
+        stores[name] += 16
+    q.wait_ge(S.sta, stores["sta"])
+    a.wait_ge(S.stb, stores["stb"])

@@ -42,6 +42,21 @@ def _count(mask):
     return bin(mask).count("1")
 
 
+def _groups(cores, topo, d):
+    n = len(cores)
+    raw = sorted((t for t in range(n) if t != d and not topo.may_write(cores[t], cores[d])), key=lambda t: (d - t) % n)
+    h = (len(raw) + 1) // 2
+    return raw[:h], raw[h:]
+
+
+def _places(cores, topo, d):
+    near, away = _groups(cores, topo, d)
+    out = []
+    for k in range(len(near)):
+        out += near[k:k + 1] + away[k:k + 1]
+    return out
+
+
 def _plan(cores, topo):
     n = len(cores)
     every = range(topo.CHIPS * topo.CORES_PER_CHIP)
@@ -51,6 +66,7 @@ def _plan(cores, topo):
         direct = [d for d in others if topo.may_write(s, cores[d])]
         far = [d for d in others if not topo.may_write(s, cores[d])]
         jobs = {}
+        split = False
         if far:
             cand = [c for c in every if topo.chip(c) == topo.chip(s) and c not in cores
                     and all(topo.may_write(c, cores[d]) for d in far)]
@@ -59,9 +75,10 @@ def _plan(cores, topo):
             units = [(p, d) for p in PARTS for d in far]
             if len(units) <= len(near):
                 use = near
-                if len(units) <= len(away) and _late(cores, topo, j, far[0]):
+                if len(units) <= len(away) and j in _groups(cores, topo, far[0])[1]:
                     use = away
                 helpers = use[:len(units)]
+                split = len(units) <= len(away)
             else:
                 helpers = []
                 for k in range(max(len(near), len(away))):
@@ -73,23 +90,41 @@ def _plan(cores, topo):
                     k, load = k + 1, 0
                 jobs.setdefault(helpers[k], {q: [] for q in PARTS})[p].append(d)
                 load += WEIGHT[p]
-        plan.append({"direct": direct, "far": far, "jobs": jobs})
+        hop1 = list(jobs)
+        parts = PARTS
+        if far and not direct:
+            parts = tuple(reversed(PARTS))
+        if far and direct:
+            place = _places(cores, topo, far[0]).index(j)
+            ports = 2 if split else 1
+            if place >= ports:
+                parts = tuple(reversed(PARTS))
+            if len(direct) > 1:
+                last = direct[-1]
+                pool = [c for c in every if topo.chip(c) == topo.chip(s) and topo.die(c) != topo.die(s)
+                        and c not in cores and c not in jobs and topo.may_write(c, cores[last])]
+                pool.sort(key=lambda c: all(topo.may_write(c, cores[d]) for d in far))
+                if len(pool) >= len(PARTS):
+                    direct = direct[:-1]
+                    fwd = pool[:len(PARTS)]
+                    for p, c in zip(PARTS, fwd):
+                        jobs[c] = {q: [] for q in PARTS}
+                        jobs[c][p].append(last)
+                    hop1 = fwd + hop1 if place >= 2 * ports else hop1 + fwd
+        plan.append({"direct": direct, "far": far, "jobs": jobs, "hop1": hop1, "parts": parts})
     return plan
 
 
-def _peers(cores, topo, d):
-    n = len(cores)
-    return sorted((t for t in range(n) if t != d and not topo.may_write(cores[t], cores[d])), key=lambda t: (d - t) % n)
-
-
-def _late(cores, topo, j, d):
-    peers = _peers(cores, topo, d)
-    return peers.index(j) >= (len(peers) + 1) // 2
-
-
 def _order(cores, topo, plan, r):
-    direct = sorted((t for t in range(len(cores)) if r in plan[t]["direct"]), key=lambda t: plan[t]["direct"].index(r))
-    return [r] + direct + _peers(cores, topo, r)
+    def whole(t):
+        k, m = plan[t]["direct"].index(r) + 1, len(plan[t]["direct"])
+        a, b = plan[t]["parts"]
+        return m * WEIGHT[a] + k * WEIGHT[b]
+    n = len(cores)
+    direct = sorted((t for t in range(n) if r in plan[t]["direct"]), key=lambda t: (whole(t), (r - t) % n))
+    across = _places(cores, topo, r)
+    fwd = [t for t in range(n) if t != r and t not in direct and t not in across]
+    return [r] + direct + fwd + across
 
 
 def rank_program(g, core, T, topo):
@@ -108,31 +143,38 @@ def rank_program(g, core, T, topo):
             m = topo.mask(src, d) if m is None else m & topo.mask(src, d)
         return m
 
-    def send(part, j, dst, mask, sem):
+    def transfer(part, j, dst, mask, sem):
         ids = []
         for d in dst:
             a = topo.addr(d)
             ids.append(DstId(rid=a[0], pnc=a[1]))
-        g.remote_dma_fused([RemoteDMATransfer(dst_ids=ids, dma_engine_mask=mask, remote_sem=sem,
-                                              srcs=[view(part, j)], dsts=[view(part, j) for d in dst])],
-                           local_sem=S.ls)
-        return _count(mask)
+        return RemoteDMATransfer(dst_ids=ids, dma_engine_mask=mask, remote_sem=sem,
+                                 srcs=[view(part, j)], dsts=[view(part, j) for d in dst])
 
     def hop1_mask(j):
         busy = 0
         for d in plan[j]["direct"]:
             busy |= topo.mask(cores[j], cores[d])
-        return common_mask(cores[j], list(plan[j]["jobs"])) & ~busy
+        return common_mask(cores[j], plan[j]["hop1"]) & ~busy
+
+    def last_mask(j, d, p):
+        if d in plan[j]["direct"]:
+            return common_mask(cores[j], [cores[e] for e in plan[j]["direct"]])
+        for h in plan[j]["jobs"]:
+            if d in plan[j]["jobs"][h][p]:
+                return common_mask(h, [cores[e] for e in plan[j]["jobs"][h][p]])
 
     for j in range(N):
         if core in plan[j]["jobs"]:
             job = plan[j]["jobs"][core]
             left = 0
-            for p in PARTS:
+            for p in plan[j]["parts"]:
                 if job[p]:
                     dst = [cores[d] for d in job[p]]
+                    m = common_mask(core, dst)
                     g.wait_ge(S.rc if p == "c" else S.rs, _count(hop1_mask(j)))
-                    left += send(p, j, dst, common_mask(core, dst), S["arr%d" % j])
+                    g.remote_dma_fused([transfer(p, j, dst, m, S["arr%d" % j])], local_sem=S.ls)
+                    left += _count(m)
             g.wait_ge(S.ls, left)
             return
 
@@ -178,14 +220,17 @@ def rank_program(g, core, T, topo):
     g.wait_ge(S.qh, 1)
     left = 0
     jobs = plan[r]["jobs"]
-    for p in PARTS:
-        to = [h for h in jobs if jobs[h][p]]
-        if to:
-            left += send(p, r, to, hop1_mask(r), S.rc if p == "c" else S.rs)
     direct = [cores[d] for d in plan[r]["direct"]]
-    if direct:
-        for p in reversed(PARTS):
-            left += send(p, r, direct, common_mask(core, direct), S["arr%d" % r])
+    for p in plan[r]["parts"]:
+        trs = []
+        to = [h for h in plan[r]["hop1"] if jobs[h][p]]
+        if to:
+            trs.append(transfer(p, r, to, hop1_mask(r), S.rc if p == "c" else S.rs))
+            left += _count(hop1_mask(r))
+        if direct:
+            trs.append(transfer(p, r, direct, common_mask(core, direct), S["arr%d" % r]))
+            left += _count(common_mask(core, direct))
+        g.remote_dma_fused(trs, local_sem=S.ls)
     g.wait_ge(S.ls, left)
 
     stores = {"sta": 0, "stb": 0}
@@ -194,12 +239,7 @@ def rank_program(g, core, T, topo):
         if j == r:
             t.wait_ge(S.qh, 1)
         else:
-            if r in plan[j]["direct"]:
-                n_in = len(PARTS) * _count(common_mask(cores[j], [cores[d] for d in plan[j]["direct"]]))
-            else:
-                n_in = sum(_count(common_mask(h, [cores[d] for d in plan[j]["jobs"][h][p]]))
-                           for h in plan[j]["jobs"] for p in PARTS if r in plan[j]["jobs"][h][p])
-            t.wait_ge(S["arr%d" % j], n_in)
+            t.wait_ge(S["arr%d" % j], sum(_count(last_mask(j, r, p)) for p in PARTS))
         slot = slice(NC * j, NC * (j + 1))
         for i in range(WT):
             b = (G + WT * k + i) % NBANK
@@ -212,17 +252,22 @@ def rank_program(g, core, T, topo):
             t.matmul_mx(bank(b), T.w2q[:, w], T.w2s[:, w], T.hq[:, slot], T.hs[:, slot], True, True
                         ).then_inc(S["n%d_%d" % (k, i)], 1)
             out = T.yb[:, NC * (WT * j + i):NC * (WT * j + i + 1)]
-            if i == 0:
-                v.wait_ge(S["n%d_%d" % (k, i)], 1)
-                v.tensor_copy(out, bank(b)).then_inc(S["c%d_%d" % (k, i)], 1)
-            else:
-                a.wait_ge(S["n%d_%d" % (k, i)], 1)
-                a.activation(out, bank(b), ActivationFunctionType.Copy).then_inc(S["c%d_%d" % (k, i)], 1)
-        e, name = (q, "sta") if k % 2 == 0 else (a, "stb")
-        for i in range(WT):
-            e.wait_ge(S["c%d_%d" % (k, i)], 1)
-        blk = slice(NC * WT * j, NC * WT * (j + 1))
-        e.dma_start(T.y[:, blk], T.yb[:, blk]).then_inc(S[name], 16)
-        stores[name] += 16
+            v.wait_ge(S["n%d_%d" % (k, i)], 1)
+            v.tensor_copy(out, bank(b)).then_inc(S["c%d_%d" % (k, i)], 1)
+        two = [(q, "sta"), (a, "stb")]
+        if k < N - 1:
+            e, name = two[k % 2]
+            for i in range(WT):
+                e.wait_ge(S["c%d_%d" % (k, i)], 1)
+            blk = slice(NC * WT * j, NC * WT * (j + 1))
+            e.dma_start(T.y[:, blk], T.yb[:, blk]).then_inc(S[name], 16)
+            stores[name] += 16
+        else:
+            for i in range(WT):
+                e, name = two[(k + i) % 2]
+                e.wait_ge(S["c%d_%d" % (k, i)], 1)
+                blk = slice(NC * (WT * j + i), NC * (WT * j + i + 1))
+                e.dma_start(T.y[:, blk], T.yb[:, blk]).then_inc(S[name], 16)
+                stores[name] += 16
     q.wait_ge(S.sta, stores["sta"])
     a.wait_ge(S.stb, stores["stb"])

from concourse.bass import DstId, RemoteDMATransfer
from concourse.mybir import dt, AluOpType, ActivationFunctionType

N = 6
NC = 128
TW = 4 * NC
G = 4
WT = 2
C = 0.037
BANK = 512
NBANK = 8

SCRATCH = {
    "xb": ("sbuf", [128, TW], "bfloat16"),
    "w1b": ("sbuf", [128, G * TW], "bfloat16"),
    "w2b": ("sbuf", [128, WT * TW], "bfloat16"),
    "hb": ("sbuf", [128, TW], "bfloat16"),
    "xq": ("sbuf", [128, NC], "float8_e4m3fn_x4"),
    "xs": ("sbuf", [128, NC], "uint8"),
    "w1q": ("sbuf", [128, G * NC], "float8_e4m3fn_x4"),
    "w1s": ("sbuf", [128, G * NC], "uint8"),
    "w2q": ("sbuf", [128, WT * NC], "float8_e4m3fn_x4"),
    "w2s": ("sbuf", [128, WT * NC], "uint8"),
    "hq": ("sbuf", [128, N * NC], "float8_e4m3fn_x4"),
    "hs": ("sbuf", [128, N * NC], "uint8"),
    "ps": ("psum", [128, NBANK * BANK], "float32"),
    "yb": ("sbuf", [128, N * WT * NC], "float32"),
}
SEMAPHORES = (
    ["lx", "lw1a", "lw1b", "lw2", "qx", "qh", "qv", "rc", "rs", "ls", "sta", "stb"]
    + ["qw%d" % i for i in range(G)] + ["m%d" % i for i in range(G)] + ["a%d" % i for i in range(G)]
    + ["arr%d" % j for j in range(N)]
    + ["n%d_%d" % (k, i) for k in range(N) for i in range(WT)]
    + ["c%d_%d" % (k, i) for k in range(N) for i in range(WT)]
)

PARTS = ("c", "s")
WEIGHT = {"c": 3, "s": 2}


def _count(mask):
    return bin(mask).count("1")


def _groups(cores, topo, d):
    n = len(cores)
    raw = sorted((t for t in range(n) if t != d and not topo.may_write(cores[t], cores[d])), key=lambda t: (d - t) % n)
    h = (len(raw) + 1) // 2
    return raw[:h], raw[h:]


def _places(cores, topo, d):
    near, away = _groups(cores, topo, d)
    out = []
    for k in range(len(near)):
        out += near[k:k + 1] + away[k:k + 1]
    return out


def _plan(cores, topo):
    n = len(cores)
    every = range(topo.CHIPS * topo.CORES_PER_CHIP)
    plan = []
    for j, s in enumerate(cores):
        others = sorted((d for d in range(n) if d != j), key=lambda d: (d - j) % n)
        direct = [d for d in others if topo.may_write(s, cores[d])]
        far = [d for d in others if not topo.may_write(s, cores[d])]
        jobs = {}
        split = False
        if far:
            cand = [c for c in every if topo.chip(c) == topo.chip(s) and c not in cores
                    and all(topo.may_write(c, cores[d]) for d in far)]
            near = [c for c in cand if topo.die(c) == topo.die(s)]
            away = [c for c in cand if topo.die(c) != topo.die(s)]
            units = [(p, d) for p in PARTS for d in far]
            if len(units) <= len(near):
                use = near
                if len(units) <= len(away) and j in _groups(cores, topo, far[0])[1]:
                    use = away
                helpers = use[:len(units)]
                split = len(units) <= len(away)
            else:
                helpers = []
                for k in range(max(len(near), len(away))):
                    helpers += near[k:k + 1] + away[k:k + 1]
            target = sum(WEIGHT[p] for p, d in units) / len(helpers)
            k, load = 0, 0
            for p, d in units:
                if k < len(helpers) - 1 and load > 0 and load + WEIGHT[p] / 2 > target:
                    k, load = k + 1, 0
                jobs.setdefault(helpers[k], {q: [] for q in PARTS})[p].append(d)
                load += WEIGHT[p]
        hop1 = list(jobs)
        parts = PARTS
        if far and not direct:
            parts = tuple(reversed(PARTS))
        if far and direct:
            place = _places(cores, topo, far[0]).index(j)
            ports = 2 if split else 1
            if place >= ports:
                parts = tuple(reversed(PARTS))
            if len(direct) > 1:
                last = direct[-1]
                pool = [c for c in every if topo.chip(c) == topo.chip(s) and topo.die(c) != topo.die(s)
                        and c not in cores and c not in jobs and topo.may_write(c, cores[last])]
                pool.sort(key=lambda c: all(topo.may_write(c, cores[d]) for d in far))
                if len(pool) >= len(PARTS):
                    direct = direct[:-1]
                    fwd = pool[:len(PARTS)]
                    for p, c in zip(PARTS, fwd):
                        jobs[c] = {q: [] for q in PARTS}
                        jobs[c][p].append(last)
                    hop1 = fwd + hop1 if place >= 2 * ports else hop1 + fwd
        plan.append({"direct": direct, "far": far, "jobs": jobs, "hop1": hop1, "parts": parts})
    return plan


def _order(cores, topo, plan, r):
    def whole(t):
        k, m = plan[t]["direct"].index(r) + 1, len(plan[t]["direct"])
        a, b = plan[t]["parts"]
        return m * WEIGHT[a] + k * WEIGHT[b]
    n = len(cores)
    direct = sorted((t for t in range(n) if r in plan[t]["direct"]), key=lambda t: (whole(t), (r - t) % n))
    across = _places(cores, topo, r)
    fwd = [t for t in range(n) if t != r and t not in direct and t not in across]
    return [r] + direct + fwd + across


def rank_program(g, core, T, topo):
    cores = [int(c) for c in T.cores]
    plan = _plan(cores, topo)
    S = T.sem

    def view(part, j):
        if part == "c":
            return T.hq[:, NC * j:NC * (j + 1)].bitcast(dt.uint8)
        return T.hs[:, NC * j:NC * (j + 1)]

    def common_mask(src, dst):
        m = None
        for d in dst:
            m = topo.mask(src, d) if m is None else m & topo.mask(src, d)
        return m

    def transfer(part, j, dst, mask, sem):
        ids = []
        for d in dst:
            a = topo.addr(d)
            ids.append(DstId(rid=a[0], pnc=a[1]))
        return RemoteDMATransfer(dst_ids=ids, dma_engine_mask=mask, remote_sem=sem,
                                 srcs=[view(part, j)], dsts=[view(part, j) for d in dst])

    def hop1_mask(j):
        busy = 0
        for d in plan[j]["direct"]:
            busy |= topo.mask(cores[j], cores[d])
        return common_mask(cores[j], plan[j]["hop1"]) & ~busy

    def last_mask(j, d, p):
        if d in plan[j]["direct"]:
            return common_mask(cores[j], [cores[e] for e in plan[j]["direct"]])
        for h in plan[j]["jobs"]:
            if d in plan[j]["jobs"][h][p]:
                return common_mask(h, [cores[e] for e in plan[j]["jobs"][h][p]])

    for j in range(N):
        if core in plan[j]["jobs"]:
            job = plan[j]["jobs"][core]
            left = 0
            for p in plan[j]["parts"]:
                if job[p]:
                    dst = [cores[d] for d in job[p]]
                    m = common_mask(core, dst)
                    g.wait_ge(S.rc if p == "c" else S.rs, _count(hop1_mask(j)))
                    g.remote_dma_fused([transfer(p, j, dst, m, S["arr%d" % j])], local_sem=S.ls)
                    left += _count(m)
            g.wait_ge(S.ls, left)
            return

    r = T.rank_of(core)
    if r is None:
        return
    v, t, a, q = g.vector, g.tensor, g.scalar, g.sync

    def bank(b):
        return T.ps[:, BANK * b:BANK * b + NC]

    head = (G - 1) * TW
    q.dma_start(T.xb[:], T.x[:]).then_inc(S.lx, 16)
    a.dma_start(T.w1b[:, 0:head], T.w1[:, 0:head]).then_inc(S.lw1a, 16)
    q.dma_start(T.w1b[:, head:G * TW], T.w1[:, head:G * TW]).then_inc(S.lw1b, 16)
    q.dma_start(T.w2b[:], T.w2[:]).then_inc(S.lw2, 16)

    v.wait_ge(S.lx, 16)
    v.quantize_mx(T.xq[:], T.xs[:], T.xb[:]).then_inc(S.qx, 1)
    t.wait_ge(S.qx, 1)
    for i in range(G):
        if i == 0:
            v.wait_ge(S.lw1a, 16)
        if i == G - 1:
            v.wait_ge(S.lw1b, 16)
        cols = slice(NC * i, NC * (i + 1))
        v.quantize_mx(T.w1q[:, cols], T.w1s[:, cols], T.w1b[:, TW * i:TW * (i + 1)]).then_inc(S["qw%d" % i], 1)
        t.wait_ge(S["qw%d" % i], 1)
        t.matmul_mx(bank(i), T.w1q[:, cols], T.w1s[:, cols], T.xq[:], T.xs[:], True, True).then_inc(S["m%d" % i], 1)
        if i < G - 1:
            a.wait_ge(S["m%d" % i], 1)
            a.activation(T.hb[:, i:TW:4], bank(i), ActivationFunctionType.Relu, scale=C).then_inc(S["a%d" % i], 1)
        else:
            v.wait_ge(S["m%d" % i], 1)
            v.tensor_scalar(T.hb[:, i:TW:4], bank(i), 0.0, C, AluOpType.max, AluOpType.mult).then_inc(S["a%d" % i], 1)
    for i in range(G):
        v.wait_ge(S["a%d" % i], 1)
    own = slice(NC * r, NC * (r + 1))
    v.quantize_mx(T.hq[:, own], T.hs[:, own], T.hb[:]).then_inc(S.qh, 1)
    v.wait_ge(S.lw2, 16)
    v.quantize_mx(T.w2q[:], T.w2s[:], T.w2b[:]).then_inc(S.qv, 1)

    g.wait_ge(S.qh, 1)
    left = 0
    jobs = plan[r]["jobs"]
    direct = [cores[d] for d in plan[r]["direct"]]
    for p in plan[r]["parts"]:
        trs = []
        to = [h for h in plan[r]["hop1"] if jobs[h][p]]
        if to:
            trs.append(transfer(p, r, to, hop1_mask(r), S.rc if p == "c" else S.rs))
            left += _count(hop1_mask(r))
        if direct:
            trs.append(transfer(p, r, direct, common_mask(core, direct), S["arr%d" % r]))
            left += _count(common_mask(core, direct))
        g.remote_dma_fused(trs, local_sem=S.ls)
    g.wait_ge(S.ls, left)

    stores = {"sta": 0, "stb": 0}
    t.wait_ge(S.qv, 1)
    for k, j in enumerate(_order(cores, topo, plan, r)):
        if j == r:
            t.wait_ge(S.qh, 1)
        else:
            t.wait_ge(S["arr%d" % j], sum(_count(last_mask(j, r, p)) for p in PARTS))
        slot = slice(NC * j, NC * (j + 1))
        for i in range(WT):
            b = (G + WT * k + i) % NBANK
            if G + WT * k + i >= NBANK:
                if WT * k + i < NBANK:
                    t.wait_ge(S["a%d" % b], 1)
                else:
                    t.wait_ge(S["c%d_%d" % ((WT * k + i - NBANK) // WT, i)], 1)
            w = slice(NC * i, NC * (i + 1))
            t.matmul_mx(bank(b), T.w2q[:, w], T.w2s[:, w], T.hq[:, slot], T.hs[:, slot], True, True
                        ).then_inc(S["n%d_%d" % (k, i)], 1)
            out = T.yb[:, NC * (WT * j + i):NC * (WT * j + i + 1)]
            v.wait_ge(S["n%d_%d" % (k, i)], 1)
            v.tensor_copy(out, bank(b)).then_inc(S["c%d_%d" % (k, i)], 1)
        two = [(q, "sta"), (a, "stb")]
        if k < N - 1:
            e, name = two[k % 2]
            for i in range(WT):
                e.wait_ge(S["c%d_%d" % (k, i)], 1)
            blk = slice(NC * WT * j, NC * WT * (j + 1))
            e.dma_start(T.y[:, blk], T.yb[:, blk]).then_inc(S[name], 16)
            stores[name] += 16
        else:
            for i in range(WT):
                e, name = two[(k + i) % 2]
                e.wait_ge(S["c%d_%d" % (k, i)], 1)
                blk = slice(NC * (WT * j + i), NC * (WT * j + i + 1))
                e.dma_start(T.y[:, blk], T.yb[:, blk]).then_inc(S[name], 16)
                stores[name] += 16
    q.wait_ge(S.sta, stores["sta"])
    a.wait_ge(S.stb, stores["stb"])
